import numpy as np
import ml_dtypes


def mxq(x, axis, fmt="e4m3"):
    dtype, down = {"e4m3": (ml_dtypes.float8_e4m3fn, 7), "e5m2": (ml_dtypes.float8_e5m2, 14)}[fmt]
    v = np.moveaxis(np.asarray(x, np.float32).astype(ml_dtypes.bfloat16).astype(np.float64), axis, -1)
    blocks = v.reshape(v.shape[:-1] + (-1, 32))
    amax = np.abs(blocks).max(-1, keepdims=True)
    byte = np.maximum(np.where(amax > 0, np.frexp(amax)[1] - 1 + 127, 0) - down, 1)
    scale = np.exp2(byte - 127.0)
    codes = (blocks / scale).astype(np.float32).astype(dtype).astype(np.float64)
    return np.moveaxis((codes * scale).reshape(v.shape), -1, axis)


WIDE = False


def mx_kscale(k):
    if not WIDE:
        return np.ones(k)
    levels = np.array([10, -10, 5, -5, 0])
    if k % 512:
        return np.exp2(np.random.permutation(np.resize(levels, k // 32))).repeat(32)
    a = np.empty((k // 512, 16))
    for p in range(k // 512):
        a[p, :8] = np.random.permutation(np.resize(levels, 8))
        for g in range(8):
            far = levels[np.abs(levels - a[p, g]) >= 10]
            a[p, g + 8] = far[np.random.randint(len(far))]
    return np.exp2(a.ravel()).repeat(32)


def f64(x):
    return np.asarray(x).astype(np.float64)


def striped(idx):
    return np.tile(idx.reshape(-1, 16).T, (8, 1)).astype(np.uint16)


def unstriped(offs):
    return offs[:16].T.reshape(-1).astype(np.int64)


def striped8(idx):
    return np.concatenate([x.reshape(-1, 16).T for x in idx]).astype(np.uint16)


def runs(offs, k):
    lists = np.stack([offs[16 * r : 16 * r + 16].T.reshape(-1) for r in range(8)]).astype(np.int64)
    return lists[np.arange(k) % 512 // 64]


def pack_weight(w):
    k, n = w.shape
    w = f64(np.asarray(w, np.float32).astype(ml_dtypes.bfloat16)).reshape(k // 32, 32, n)
    amax = np.abs(w).max(1)
    byte = np.clip(np.where(amax > 0, np.frexp(amax)[1] - 1 + 127 - 7, 1), 1, 254)
    scaled = (w * np.exp2(127.0 - byte)[:, None, :]).reshape(k, n).astype(np.float32)
    words = np.ascontiguousarray(scaled.reshape(k // 512, 128, 4, n).transpose(0, 1, 3, 2)).astype(ml_dtypes.float8_e4m3fn).view(np.uint8)
    return words, np.ascontiguousarray(byte.astype(np.uint8).reshape(k // 512, 16, n))


def unpack_weight(words, scales):
    g, p, n, _ = words.shape
    vals = np.ascontiguousarray(words).view(ml_dtypes.float8_e4m3fn).astype(np.float64) * np.repeat(np.exp2(scales.astype(np.float64) - 127.0), 8, axis=1)[..., None]
    return vals.transpose(0, 1, 3, 2).reshape(g * 512, n)


def sigmoid(v):
    return 1.0 / (1.0 + np.exp(-np.maximum(v, -700.0)))


K, T, S, N, H = 512, 2048, 512, 512, 512


def setup_inputs():
    n = np.random.standard_normal
    s = mx_kscale(K)[:, None]
    u = mx_kscale(H)
    packed_xT = pack_weight(n((K, T)) * s)
    return {
        "x_words": packed_xT[0],
        "x_scales": packed_xT[1],
        "w1": (n((K, H)) / np.sqrt(K) / s).astype(np.float32),
        "w2": (n((K, H)) / np.sqrt(K) / s).astype(np.float32),
        "gn": (np.random.uniform(0.5, 1.5, (H, 1)) * u[:, None]).astype(np.float32),
        "w3": (n((H, N)) / np.sqrt(H) / u[:, None]).astype(np.float32),
        "offs": striped(np.random.permutation(T)[:S]),
        "two": striped(np.random.permutation(T)[:S]),
        "n1": striped8(np.stack([np.random.permutation(S) for _ in range(8)])),
        "n2": striped8(np.stack([np.random.permutation(S) for _ in range(8)])),
        "n3": striped8(np.stack([np.random.permutation(S) for _ in range(8)])),
        "n4": striped8(np.stack([np.random.permutation(S) for _ in range(8)])),
    }


def reference(x_words, x_scales, w1, w2, gn, w3, offs, two, n1, n2, n3, n4):
    xq = unpack_weight(x_words, x_scales)[:, unstriped(offs)]
    y = mxq(f64(w1), 0, "e4m3").T @ xq
    x_two = unpack_weight(x_words, x_scales)[:, unstriped(two)]
    d = mxq(f64(w2), 0, "e4m3").T @ x_two
    z = f64(gn) * (0.75 * (y * (d[np.arange(H)[:, None], runs(n2, H)]) - ((y[np.arange(H)[:, None], runs(n1, H)]) * d)))
    h = mxq(f64(w3), 0, "e4m3").T @ mxq(z, 0, "e4m3")
    st = h[np.arange(N)[:, None], runs(n3, N)] - h
    return h * (sigmoid(st[np.arange(N)[:, None], runs(n4, N)]))

@@ -1,0 +1,194 @@
+from contextlib import ExitStack
+
+import concourse.mybir as mybir
+
+K, T, S, H, N = 512, 2048, 512, 512, 512
+FLOPS = 2 * (2 * K * H * S + H * N * S)
+
+F32 = mybir.dt.float32
+BF16 = mybir.dt.bfloat16
+I32 = mybir.dt.int32
+U32 = mybir.dt.uint32
+U16 = mybir.dt.uint16
+U8 = mybir.dt.uint8
+FP8X4 = mybir.dt.float8_e4m3fn_x4
+MULT = mybir.AluOpType.mult
+SUBTRACT = mybir.AluOpType.subtract
+COPY = mybir.ActivationFunctionType.Copy
+SIGMOID = mybir.ActivationFunctionType.Sigmoid
+
+P = 128
+PACK = 4
+HALF = S // 2
+LIST_ROWS = 16
+
+
+def tile_picked_twlcrossbhopd_none_p_kernel(tc, x_words, x_scales, w1, w2, gn, w3, offs, two, n1, n2, n3, n4, out):
+    nc = tc.nc
+    with ExitStack() as ctx:
+        keep = ctx.enter_context(tc.tile_pool(name="keep", bufs=1))
+        psum = ctx.enter_context(tc.psum_pool(name="psum", bufs=1))
+
+        def load_list(name, dram):
+            tile = keep.tile([P, S // LIST_ROWS], U16, name=name)
+            nc.sync.dma_start(tile[:], dram)
+            return tile
+
+        def load_weight(name, dram):
+            tile = keep.tile([P, PACK, H], F32, name=name)
+            nc.sync.dma_start(tile[:], dram.rearrange("(p j) c -> p j c", j=PACK))
+            return tile
+
+        def entries(list_tile, half):
+            cols = HALF // LIST_ROWS
+            return list_tile[:, half * cols : (half + 1) * cols]
+
+        def places(half):
+            return slice(half * HALF, (half + 1) * HALF)
+
+        table_scales = keep.tile([P, T], U8, name="table_scales")
+        nc.vector.memset(table_scales[:].bitcast(I32), 0)
+        for q in range(4):
+            nc.scalar.dma_start(table_scales[32 * q : 32 * q + 4, :].bitcast(I32), x_scales[0, 4 * q : 4 * q + 4, :].bitcast(I32))
+
+        warm = keep.tile([P, 1], F32, name="warm")
+        nc.vector.memset(warm[:], 0.0)
+        warmed = keep.tile([P, 1], F32, name="warmed")
+        nc.scalar.activation(warmed[:], warm[:], SIGMOID)
+
+        offs_sb = load_list("offs_sb", offs)
+        two_sb = load_list("two_sb", two)
+        table_words = keep.tile([P, T], I32, name="table_words")
+        nc.sync.dma_start(table_words[:], x_words[0].rearrange("p c r -> p (c r)").bitcast(I32))
+        w1_raw = load_weight("w1_raw", w1)
+        w2_raw = load_weight("w2_raw", w2)
+        n1_sb = load_list("n1_sb", n1)
+        n2_sb = load_list("n2_sb", n2)
+        gain = keep.tile([P, PACK], F32, name="gain")
+        nc.sync.dma_start(gain[:], gn.rearrange("(p t) o -> p (t o)", t=PACK))
+        w3_raw = load_weight("w3_raw", w3)
+        n3_sb = load_list("n3_sb", n3)
+        n4_sb = load_list("n4_sb", n4)
+
+        def gather_words(name, list_tile):
+            tile = keep.tile([P, S], U32, name=name, align_bytes=64)
+            nc.vector.tensor_copy(tile[:], table_words[:].bitcast(U32).indirect(list_tile[:]))
+            return tile
+
+        def gather_scales(name, list_tile):
+            tile = keep.tile([P, S], U8, name=name, align_bytes=64)
+            nc.vector.tensor_copy(tile[:], table_scales[:].indirect(list_tile[:]))
+            return tile
+
+        def round_pair(name, raw, pair, copy):
+            tile = keep.tile([P, 2, P * PACK], BF16, name=name, align_bytes=64)
+            copy(
+                tile[:].rearrange("p t (m j) -> p m j t", j=PACK),
+                raw[:].rearrange("p j (m t) -> p m j t", t=PACK)[:, :, :, 2 * pair : 2 * pair + 2],
+            )
+            return tile
+
+        def quantize(name, values, width):
+            codes = keep.tile([P, width], U32, name=name + "_codes", align_bytes=64)
+            scales = keep.tile([P, width], U8, name=name + "_scales", align_bytes=64)
+            nc.vector.quantize_mx(codes[:].bitcast(FP8X4), scales[:], values)
+            return codes, scales
+
+        def quantize_pair(name, rounded):
+            codes, scales = quantize(name, rounded[:].rearrange("p t c -> p (t c)"), 2 * P)
+            return [(codes[:, u * P : (u + 1) * P], scales[:, u * P : (u + 1) * P]) for u in range(2)]
+
+        def product(bank, weight, codes, scales):
+            nc.tensor.matmul_mx(bank, weight[0].bitcast(FP8X4), weight[1], codes.bitcast(FP8X4), scales, start=True, stop=True)
+
+        offs_words = gather_words("offs_words", offs_sb)
+        two_words = gather_words("two_words", two_sb)
+        offs_scales = gather_scales("offs_scales", offs_sb)
+        w1_rounded = [round_pair("w1_rounded%d" % pair, w1_raw, pair, nc.scalar.copy) for pair in range(2)]
+        w1_mx = quantize_pair("w1_0", w1_rounded[0])
+        two_scales = gather_scales("two_scales", two_sb)
+
+        y_sb = [keep.tile([P, S], F32, name="y%d" % t) for t in range(PACK)]
+        d_sb = [keep.tile([P, S], F32, name="d%d" % t) for t in range(PACK)]
+
+        def project_y(t):
+            bank = psum.tile([P, S], F32, name="bank%d" % t)
+            product(bank[:], w1_mx[t], offs_words[:], offs_scales[:])
+            nc.scalar.activation(y_sb[t][:], bank[:], COPY, scale=gain[:, t : t + 1])
+
+        def project_d(t):
+            bank = psum.tile([P, S], F32, name="bank%d" % (PACK + t))
+            product(bank[:], w2_mx[t], two_words[:], two_scales[:])
+            nc.scalar.activation(d_sb[t][:], bank[:], COPY, scale=0.75)
+
+        project_y(0)
+        w2_first = round_pair("w2_rounded0", w2_raw, 0, nc.vector.tensor_copy)
+        w2_mx = quantize_pair("w2_0", w2_first)
+        project_d(0)
+        project_y(1)
+        project_d(1)
+        w2_second = round_pair("w2_rounded1", w2_raw, 1, nc.vector.tensor_copy)
+        w1_mx.extend(quantize_pair("w1_1", w1_rounded[1]))
+        w2_mx.extend(quantize_pair("w2_1", w2_second))
+        for t in range(2, PACK):
+            project_y(t)
+            project_d(t)
+
+        w3_rounded = [round_pair("w3_rounded%d" % pair, w3_raw, pair, nc.scalar.copy) for pair in range(2)]
+        w3_mx = []
+
+        h_sb = [keep.tile([P, S], F32, name="h%d" % t) for t in range(PACK)]
+        h_plain = [keep.tile([P, S], F32, name="h_plain%d" % t) for t in range(PACK)]
+
+        def cross(half):
+            left = keep.tile([P, PACK, HALF], F32, name="left%d" % half)
+            right = keep.tile([P, PACK, HALF], F32, name="right%d" % half)
+            for t in range(PACK):
+                nc.vector.tensor_tensor(left[:, t, :], d_sb[t][:].indirect(entries(n2_sb, half)), y_sb[t][:, places(half)], MULT)
+                nc.vector.tensor_tensor(right[:, t, :], y_sb[t][:].indirect(entries(n1_sb, half)), d_sb[t][:, places(half)], MULT)
+            z = keep.tile([P, HALF, PACK], BF16, name="z%d" % half, align_bytes=64)
+            nc.vector.tensor_tensor(
+                z[:].rearrange("p (c i) t -> p c t i", i=4),
+                left[:].rearrange("p t (c i) -> p c t i", i=4),
+                right[:].rearrange("p t (c i) -> p c t i", i=4),
+                SUBTRACT,
+            )
+            return z
+
+        def project_h(half, z):
+            codes, scales = quantize("z%d" % half, z[:].rearrange("p c t -> p (c t)"), HALF)
+            for t in range(PACK):
+                bank = psum.tile([P, HALF], F32, name="bank%d" % (half * PACK + t))
+                product(bank[:], w3_mx[t], codes[:], scales[:])
+                nc.scalar.copy(h_sb[t][:, places(half)], bank[:])
+                nc.scalar.copy(h_plain[t][:, places(half)], bank[:])
+
+        z_first = cross(0)
+        for pair in range(2):
+            w3_mx.extend(quantize_pair("w3_%d" % pair, w3_rounded[pair]))
+        project_h(0, z_first)
+        project_h(1, cross(1))
+
+        out_rows = out.rearrange("(p t) s -> p t s", t=PACK)
+        gates = {}
+
+        def hop(t):
+            st = keep.tile([P, S], F32, name="st%d" % t)
+            for half in range(2):
+                nc.vector.tensor_tensor(st[:, places(half)], h_sb[t][:].indirect(entries(n3_sb, half)), h_plain[t][:, places(half)], SUBTRACT)
+            for half in range(2):
+                gate = keep.tile([P, HALF], F32, name="gate%d_%d" % (t, half))
+                nc.scalar.activation(gate[:], st[:].indirect(entries(n4_sb, half)), SIGMOID)
+                gates[(t, half)] = gate
+
+        def finish(t):
+            for half in range(2):
+                result = keep.tile([P, HALF], F32, name="result%d_%d" % (t, half))
+                nc.vector.tensor_tensor(result[:], gates[(t, half)][:], h_plain[t][:, places(half)], MULT)
+                nc.sync.dma_start(out_rows[:, t, places(half)], result[:])
+
+        hop(0)
+        for t in range(1, PACK):
+            hop(t)
+            finish(t - 1)
+        finish(PACK - 1)

@@ -21,6 +21,10 @@ P = 128
 PACK = 4
 HALF = S // 2
 LIST_ROWS = 16
+CHUNKS = [(0, 384), (384, 128)]
+Y_BANKS = "aabc"
+D_BANKS = "bcde"
+H_BANKS = ["aceg", "bdfh"]
 
 
 def tile_picked_twlcrossbhopd_none_p_kernel(tc, x_words, x_scales, w1, w2, gn, w3, offs, two, n1, n2, n3, n4, out):
@@ -35,7 +39,7 @@ def tile_picked_twlcrossbhopd_none_p_kernel(tc, x_words, x_scales, w1, w2, gn, w
             return tile
 
         def load_weight(name, dram):
-            tile = keep.tile([P, PACK, H], F32, name=name)
+            tile = keep.tile([P, PACK, H], F32, name=name, align_bytes=64)
             nc.sync.dma_start(tile[:], dram.rearrange("(p j) c -> p j c", j=PACK))
             return tile
 
@@ -58,14 +62,14 @@ def tile_picked_twlcrossbhopd_none_p_kernel(tc, x_words, x_scales, w1, w2, gn, w
 
         offs_sb = load_list("offs_sb", offs)
         two_sb = load_list("two_sb", two)
+        w1_raw = load_weight("w1_raw", w1)
         table_words = keep.tile([P, T], I32, name="table_words")
         nc.sync.dma_start(table_words[:], x_words[0].rearrange("p c r -> p (c r)").bitcast(I32))
-        w1_raw = load_weight("w1_raw", w1)
-        w2_raw = load_weight("w2_raw", w2)
+        w2_raw = load_weight("y0", w2)
         n1_sb = load_list("n1_sb", n1)
         n2_sb = load_list("n2_sb", n2)
         gain = keep.tile([P, PACK], F32, name="gain")
-        nc.sync.dma_start(gain[:], gn.rearrange("(p t) o -> p (t o)", t=PACK))
+        nc.gpsimd.dma_start(gain[:], gn.rearrange("(p t) o -> p (t o)", t=PACK))
         w3_raw = load_weight("w3_raw", w3)
         n3_sb = load_list("n3_sb", n3)
         n4_sb = load_list("n4_sb", n4)
@@ -101,52 +105,65 @@ def tile_picked_twlcrossbhopd_none_p_kernel(tc, x_words, x_scales, w1, w2, gn, w
         def product(bank, weight, codes, scales):
             nc.tensor.matmul_mx(bank, weight[0].bitcast(FP8X4), weight[1], codes.bitcast(FP8X4), scales, start=True, stop=True)
 
-        offs_words = gather_words("offs_words", offs_sb)
-        two_words = gather_words("two_words", two_sb)
         offs_scales = gather_scales("offs_scales", offs_sb)
-        w1_rounded = [round_pair("w1_rounded%d" % pair, w1_raw, pair, nc.scalar.copy) for pair in range(2)]
-        w1_mx = quantize_pair("w1_0", w1_rounded[0])
         two_scales = gather_scales("two_scales", two_sb)
+        w1_mx = []
+        for pair in range(2):
+            w1_mx.extend(quantize_pair("w1_%d" % pair, round_pair("w1_rounded%d" % pair, w1_raw, pair, nc.scalar.copy)))
+        two_words = gather_words("two_words", two_sb)
+        offs_words = gather_words("offs_words", offs_sb)
+        w2_first = round_pair("w2_rounded0", w2_raw, 0, nc.scalar.copy)
+        w2_second = round_pair("w2_rounded1", w2_raw, 1, nc.vector.tensor_copy)
 
-        y_sb = [keep.tile([P, S], F32, name="y%d" % t) for t in range(PACK)]
+        y_sb = [keep.tile([P, S], F32, name="y%d" % t, align_bytes=64) for t in range(PACK)]
         d_sb = [keep.tile([P, S], F32, name="d%d" % t) for t in range(PACK)]
 
         def project_y(t):
-            bank = psum.tile([P, S], F32, name="bank%d" % t)
+            bank = psum.tile([P, S], F32, name="bank_" + Y_BANKS[t])
             product(bank[:], w1_mx[t], offs_words[:], offs_scales[:])
             nc.scalar.activation(y_sb[t][:], bank[:], COPY, scale=gain[:, t : t + 1])
 
         def project_d(t):
-            bank = psum.tile([P, S], F32, name="bank%d" % (PACK + t))
+            bank = psum.tile([P, S], F32, name="bank_" + D_BANKS[t])
             product(bank[:], w2_mx[t], two_words[:], two_scales[:])
             nc.scalar.activation(d_sb[t][:], bank[:], COPY, scale=0.75)
 
         project_y(0)
-        w2_first = round_pair("w2_rounded0", w2_raw, 0, nc.vector.tensor_copy)
-        w2_mx = quantize_pair("w2_0", w2_first)
+        w2_mx = []
+        for t in range(2):
+            codes, scales = quantize("w2_0_%d" % t, w2_first[:, t, :], P)
+            w2_mx.append((codes[:], scales[:]))
         project_d(0)
         project_y(1)
         project_d(1)
-        w2_second = round_pair("w2_rounded1", w2_raw, 1, nc.vector.tensor_copy)
-        w1_mx.extend(quantize_pair("w1_1", w1_rounded[1]))
         w2_mx.extend(quantize_pair("w2_1", w2_second))
         for t in range(2, PACK):
             project_y(t)
             project_d(t)
 
-        w3_rounded = [round_pair("w3_rounded%d" % pair, w3_raw, pair, nc.scalar.copy) for pair in range(2)]
+        w3_rounded = keep.tile([P, PACK, P * PACK], BF16, name="w3_rounded", tag="two_words", align_bytes=64)
+        nc.scalar.copy(
+            w3_rounded[:].rearrange("p t (m j) -> p m j t", j=PACK),
+            w3_raw[:].rearrange("p j (m t) -> p m j t", t=PACK),
+        )
         w3_mx = []
 
         h_sb = [keep.tile([P, S], F32, name="h%d" % t) for t in range(PACK)]
         h_plain = [keep.tile([P, S], F32, name="h_plain%d" % t) for t in range(PACK)]
 
-        def cross(half):
-            left = keep.tile([P, PACK, HALF], F32, name="left%d" % half)
-            right = keep.tile([P, PACK, HALF], F32, name="right%d" % half)
+        def cross(chunk):
+            first, width = CHUNKS[chunk]
+            cols = slice(first, first + width)
+            list_cols = slice(first // LIST_ROWS, (first + width) // LIST_ROWS)
+            left = keep.tile([P, PACK, width], F32, name="left")
+            right = keep.tile([P, PACK, width], F32, name="right")
             for t in range(PACK):
-                nc.vector.tensor_tensor(left[:, t, :], d_sb[t][:].indirect(entries(n2_sb, half)), y_sb[t][:, places(half)], MULT)
-                nc.vector.tensor_tensor(right[:, t, :], y_sb[t][:].indirect(entries(n1_sb, half)), d_sb[t][:, places(half)], MULT)
-            z = keep.tile([P, HALF, PACK], BF16, name="z%d" % half, align_bytes=64)
+                nc.vector.tensor_tensor(left[:, t, :], d_sb[t][:].indirect(n2_sb[:, list_cols]), y_sb[t][:, cols], MULT)
+                nc.vector.tensor_tensor(right[:, t, :], y_sb[t][:].indirect(n1_sb[:, list_cols]), d_sb[t][:, cols], MULT)
+            return left, right
+
+        def difference(chunk, left, right):
+            z = keep.tile([P, CHUNKS[chunk][1], PACK], BF16, name="z%d" % chunk, tag=["two_words", "z1"][chunk], align_bytes=64)
             nc.vector.tensor_tensor(
                 z[:].rearrange("p (c i) t -> p c t i", i=4),
                 left[:].rearrange("p t (c i) -> p c t i", i=4),
@@ -155,19 +172,24 @@ def tile_picked_twlcrossbhopd_none_p_kernel(tc, x_words, x_scales, w1, w2, gn, w
             )
             return z
 
-        def project_h(half, z):
-            codes, scales = quantize("z%d" % half, z[:].rearrange("p c t -> p (c t)"), HALF)
+        def project_h(chunk, z):
+            first, width = CHUNKS[chunk]
+            pieces = [(0, 256), (256, 128)] if width == 384 else [(0, width)]
+            z_mx = []
+            for start, size in pieces:
+                z_mx.append(quantize("z%d_%d" % (chunk, start), z[:, start : start + size, :].rearrange("p c t -> p (c t)"), size))
             for t in range(PACK):
-                bank = psum.tile([P, HALF], F32, name="bank%d" % (half * PACK + t))
-                product(bank[:], w3_mx[t], codes[:], scales[:])
-                nc.scalar.copy(h_sb[t][:, places(half)], bank[:])
-                nc.scalar.copy(h_plain[t][:, places(half)], bank[:])
+                bank = psum.tile([P, width], F32, name="bank_" + H_BANKS[chunk][t])
+                for (start, size), (codes, scales) in zip(pieces, z_mx):
+                    product(bank[:, start : start + size], w3_mx[t], codes[:], scales[:])
+                nc.scalar.copy(h_sb[t][:, first : first + width], bank[:])
+                nc.scalar.copy(h_plain[t][:, first : first + width], bank[:])
 
-        z_first = cross(0)
-        for pair in range(2):
-            w3_mx.extend(quantize_pair("w3_%d" % pair, w3_rounded[pair]))
-        project_h(0, z_first)
-        project_h(1, cross(1))
+        products = cross(0)
+        w3_codes, w3_scales = quantize("w3", w3_rounded[:].rearrange("p t c -> p (t c)"), PACK * P)
+        w3_mx.extend([(w3_codes[:, t * P : (t + 1) * P], w3_scales[:, t * P : (t + 1) * P]) for t in range(PACK)])
+        project_h(0, difference(0, *products))
+        project_h(1, difference(1, *cross(1)))
 
         out_rows = out.rearrange("(p t) s -> p t s", t=PACK)
         gates = {}
@@ -176,16 +198,16 @@ def tile_picked_twlcrossbhopd_none_p_kernel(tc, x_words, x_scales, w1, w2, gn, w
             st = keep.tile([P, S], F32, name="st%d" % t)
             for half in range(2):
                 nc.vector.tensor_tensor(st[:, places(half)], h_sb[t][:].indirect(entries(n3_sb, half)), h_plain[t][:, places(half)], SUBTRACT)
+            gate = keep.tile([P, S], F32, name="gate%d" % t)
             for half in range(2):
-                gate = keep.tile([P, HALF], F32, name="gate%d_%d" % (t, half))
-                nc.scalar.activation(gate[:], st[:].indirect(entries(n4_sb, half)), SIGMOID)
-                gates[(t, half)] = gate
+                nc.scalar.activation(gate[:, places(half)], st[:].indirect(entries(n4_sb, half)), SIGMOID)
+            gates[t] = gate
 
         def finish(t):
-            for half in range(2):
-                result = keep.tile([P, HALF], F32, name="result%d_%d" % (t, half))
-                nc.vector.tensor_tensor(result[:], gates[(t, half)][:], h_plain[t][:, places(half)], MULT)
-                nc.sync.dma_start(out_rows[:, t, places(half)], result[:])
+            result = keep.tile([P, S], F32, name="result%d" % t)
+            for cols in [slice(0, S)] if t < PACK - 1 else [places(0), places(1)]:
+                nc.vector.tensor_tensor(result[:, cols], gates[t][:, cols], h_plain[t][:, cols], MULT)
+                nc.sync.dma_start(out_rows[:, t, cols], result[:, cols])
 
         hop(0)
         for t in range(1, PACK):

@@ -21,7 +21,6 @@ P = 128
 PACK = 4
 HALF = S // 2
 LIST_ROWS = 16
-CHUNKS = [(0, 384), (384, 128)]
 Y_BANKS = "aabc"
 D_BANKS = "bcde"
 H_BANKS = ["aceg", "bdfh"]
@@ -39,7 +38,7 @@ def tile_picked_twlcrossbhopd_none_p_kernel(tc, x_words, x_scales, w1, w2, gn, w
             return tile
 
         def load_weight(name, dram):
-            tile = keep.tile([P, PACK, H], F32, name=name, align_bytes=64)
+            tile = keep.tile([P, PACK, H], F32, name=name)
             nc.sync.dma_start(tile[:], dram.rearrange("(p j) c -> p j c", j=PACK))
             return tile
 
@@ -50,7 +49,7 @@ def tile_picked_twlcrossbhopd_none_p_kernel(tc, x_words, x_scales, w1, w2, gn, w
         def places(half):
             return slice(half * HALF, (half + 1) * HALF)
 
-        table_scales = keep.tile([P, T], U8, name="table_scales")
+        table_scales = keep.tile([P, T], U8, name="table_scales", align_bytes=64)
         nc.vector.memset(table_scales[:].bitcast(I32), 0)
         for q in range(4):
             nc.scalar.dma_start(table_scales[32 * q : 32 * q + 4, :].bitcast(I32), x_scales[0, 4 * q : 4 * q + 4, :].bitcast(I32))
@@ -60,17 +59,16 @@ def tile_picked_twlcrossbhopd_none_p_kernel(tc, x_words, x_scales, w1, w2, gn, w
         warmed = keep.tile([P, 1], F32, name="warmed")
         nc.scalar.activation(warmed[:], warm[:], SIGMOID)
 
+        table_words = keep.tile([P, T], I32, name="table_words")
+        nc.sync.dma_start(table_words[:], x_words[0].rearrange("p c r -> p (c r)").bitcast(I32))
         offs_sb = load_list("offs_sb", offs)
         two_sb = load_list("two_sb", two)
         w1_raw = load_weight("w1_raw", w1)
-        table_words = keep.tile([P, T], I32, name="table_words")
-        nc.sync.dma_start(table_words[:], x_words[0].rearrange("p c r -> p (c r)").bitcast(I32))
-        w2_raw = load_weight("y0", w2)
+        w2_raw = load_weight("w2_raw", w2)
         n1_sb = load_list("n1_sb", n1)
         n2_sb = load_list("n2_sb", n2)
         gain = keep.tile([P, PACK], F32, name="gain")
-        nc.gpsimd.dma_start(gain[:], gn.rearrange("(p t) o -> p (t o)", t=PACK))
-        w3_raw = load_weight("w3_raw", w3)
+        nc.sync.dma_start(gain[:], gn.rearrange("(p t) o -> p (t o)", t=PACK))
         n3_sb = load_list("n3_sb", n3)
         n4_sb = load_list("n4_sb", n4)
 
@@ -92,30 +90,35 @@ def tile_picked_twlcrossbhopd_none_p_kernel(tc, x_words, x_scales, w1, w2, gn, w
             )
             return tile
 
-        def quantize(name, values, width):
-            codes = keep.tile([P, width], U32, name=name + "_codes", align_bytes=64)
-            scales = keep.tile([P, width], U8, name=name + "_scales", align_bytes=64)
-            nc.vector.quantize_mx(codes[:].bitcast(FP8X4), scales[:], values)
-            return codes, scales
+        def quantize(name, values, scales):
+            codes = keep.tile([P, scales.shape[1]], U32, name=name, align_bytes=64)
+            nc.vector.quantize_mx(codes[:].bitcast(FP8X4), scales, values)
+            return codes
 
-        def quantize_pair(name, rounded):
-            codes, scales = quantize(name, rounded[:].rearrange("p t c -> p (t c)"), 2 * P)
-            return [(codes[:, u * P : (u + 1) * P], scales[:, u * P : (u + 1) * P]) for u in range(2)]
+        def quantize_tiles(name, rounded, scales):
+            codes = quantize(name, rounded.rearrange("p t c -> p (t c)"), scales)
+            return [(codes[:, u * P : (u + 1) * P], scales[:, u * P : (u + 1) * P]) for u in range(rounded.shape[1])]
 
         def product(bank, weight, codes, scales):
             nc.tensor.matmul_mx(bank, weight[0].bitcast(FP8X4), weight[1], codes.bitcast(FP8X4), scales, start=True, stop=True)
 
+        offs_words = gather_words("offs_words", offs_sb)
+        two_words = gather_words("two_words", two_sb)
         offs_scales = gather_scales("offs_scales", offs_sb)
         two_scales = gather_scales("two_scales", two_sb)
+        w1_rounded = [round_pair("w1_rounded%d" % pair, w1_raw, pair, nc.scalar.copy) for pair in range(2)]
+        w2_first = round_pair("w2_rounded0", w2_raw, 0, nc.scalar.copy)
+        weight_scales = keep.tile([P, 2, H], U8, name="weight_scales", tag="table_scales", align_bytes=64)
         w1_mx = []
         for pair in range(2):
-            w1_mx.extend(quantize_pair("w1_%d" % pair, round_pair("w1_rounded%d" % pair, w1_raw, pair, nc.scalar.copy)))
-        two_words = gather_words("two_words", two_sb)
-        offs_words = gather_words("offs_words", offs_sb)
-        w2_first = round_pair("w2_rounded0", w2_raw, 0, nc.scalar.copy)
-        w2_second = round_pair("w2_rounded1", w2_raw, 1, nc.vector.tensor_copy)
+            w1_mx.extend(quantize_tiles("w1_codes%d" % pair, w1_rounded[pair][:], weight_scales[:, 0, 2 * pair * P : 2 * (pair + 1) * P]))
+        w2_mx = []
+        for t in range(2):
+            w2_mx.extend(quantize_tiles("w2_codes%d" % t, w2_first[:, t : t + 1, :], weight_scales[:, 1, t * P : (t + 1) * P]))
+        w2_second = round_pair("w2_rounded0", w2_raw, 1, nc.vector.tensor_copy)
+        w2_mx.extend(quantize_tiles("w2_codes2", w2_second[:], weight_scales[:, 1, 2 * P :]))
 
-        y_sb = [keep.tile([P, S], F32, name="y%d" % t, align_bytes=64) for t in range(PACK)]
+        y_sb = [keep.tile([P, S], F32, name="y%d" % t) for t in range(PACK)]
         d_sb = [keep.tile([P, S], F32, name="d%d" % t) for t in range(PACK)]
 
         def project_y(t):
@@ -128,19 +131,11 @@ def tile_picked_twlcrossbhopd_none_p_kernel(tc, x_words, x_scales, w1, w2, gn, w
             product(bank[:], w2_mx[t], two_words[:], two_scales[:])
             nc.scalar.activation(d_sb[t][:], bank[:], COPY, scale=0.75)
 
-        project_y(0)
-        w2_mx = []
-        for t in range(2):
-            codes, scales = quantize("w2_0_%d" % t, w2_first[:, t, :], P)
-            w2_mx.append((codes[:], scales[:]))
-        project_d(0)
-        project_y(1)
-        project_d(1)
-        w2_mx.extend(quantize_pair("w2_1", w2_second))
-        for t in range(2, PACK):
+        for t in range(PACK):
             project_y(t)
             project_d(t)
 
+        w3_raw = load_weight("w1_raw", w3)
         w3_rounded = keep.tile([P, PACK, P * PACK], BF16, name="w3_rounded", tag="two_words", align_bytes=64)
         nc.scalar.copy(
             w3_rounded[:].rearrange("p t (m j) -> p m j t", j=PACK),
@@ -151,19 +146,18 @@ def tile_picked_twlcrossbhopd_none_p_kernel(tc, x_words, x_scales, w1, w2, gn, w
         h_sb = [keep.tile([P, S], F32, name="h%d" % t) for t in range(PACK)]
         h_plain = [keep.tile([P, S], F32, name="h_plain%d" % t) for t in range(PACK)]
 
-        def cross(chunk):
-            first, width = CHUNKS[chunk]
-            cols = slice(first, first + width)
-            list_cols = slice(first // LIST_ROWS, (first + width) // LIST_ROWS)
-            left = keep.tile([P, PACK, width], F32, name="left")
-            right = keep.tile([P, PACK, width], F32, name="right")
-            for t in range(PACK):
-                nc.vector.tensor_tensor(left[:, t, :], d_sb[t][:].indirect(n2_sb[:, list_cols]), y_sb[t][:, cols], MULT)
-                nc.vector.tensor_tensor(right[:, t, :], y_sb[t][:].indirect(n1_sb[:, list_cols]), d_sb[t][:, cols], MULT)
-            return left, right
-
-        def difference(chunk, left, right):
-            z = keep.tile([P, CHUNKS[chunk][1], PACK], BF16, name="z%d" % chunk, tag=["two_words", "z1"][chunk], align_bytes=64)
+        def cross(half):
+            left = keep.tile([P, PACK, HALF], F32, name="left%d" % half)
+            right = keep.tile([P, PACK, HALF], F32, name="right%d" % half, tag=["right0", "two_words"][half], align_bytes=64)
+            steps = [(t, side) for t in range(PACK) for side in range(2)]
+            if half == 1:
+                steps = [(t, side) for side in range(2) for t in range(PACK)]
+            for t, side in steps:
+                if side == 0:
+                    nc.vector.tensor_tensor(left[:, t, :], d_sb[t][:].indirect(entries(n2_sb, half)), y_sb[t][:, places(half)], MULT)
+                else:
+                    nc.vector.tensor_tensor(right[:, t, :], y_sb[t][:].indirect(entries(n1_sb, half)), d_sb[t][:, places(half)], MULT)
+            z = keep.tile([P, HALF, PACK], BF16, name="z%d" % half, align_bytes=64)
             nc.vector.tensor_tensor(
                 z[:].rearrange("p (c i) t -> p c t i", i=4),
                 left[:].rearrange("p t (c i) -> p c t i", i=4),
@@ -172,24 +166,20 @@ def tile_picked_twlcrossbhopd_none_p_kernel(tc, x_words, x_scales, w1, w2, gn, w
             )
             return z
 
-        def project_h(chunk, z):
-            first, width = CHUNKS[chunk]
-            pieces = [(0, 256), (256, 128)] if width == 384 else [(0, width)]
-            z_mx = []
-            for start, size in pieces:
-                z_mx.append(quantize("z%d_%d" % (chunk, start), z[:, start : start + size, :].rearrange("p c t -> p (c t)"), size))
+        def project_h(half, z):
+            scales = keep.tile([P, HALF], U8, name="z_scales%d" % half, align_bytes=64)
+            codes = quantize("z_codes%d" % half, z[:].rearrange("p c t -> p (c t)"), scales[:])
             for t in range(PACK):
-                bank = psum.tile([P, width], F32, name="bank_" + H_BANKS[chunk][t])
-                for (start, size), (codes, scales) in zip(pieces, z_mx):
-                    product(bank[:, start : start + size], w3_mx[t], codes[:], scales[:])
-                nc.scalar.copy(h_sb[t][:, first : first + width], bank[:])
-                nc.scalar.copy(h_plain[t][:, first : first + width], bank[:])
+                bank = psum.tile([P, HALF], F32, name="bank_" + H_BANKS[half][t])
+                product(bank[:], w3_mx[t], codes[:], scales[:])
+                nc.scalar.copy(h_sb[t][:, places(half)], bank[:])
+                nc.scalar.copy(h_plain[t][:, places(half)], bank[:])
 
-        products = cross(0)
-        w3_codes, w3_scales = quantize("w3", w3_rounded[:].rearrange("p t c -> p (t c)"), PACK * P)
-        w3_mx.extend([(w3_codes[:, t * P : (t + 1) * P], w3_scales[:, t * P : (t + 1) * P]) for t in range(PACK)])
-        project_h(0, difference(0, *products))
-        project_h(1, difference(1, *cross(1)))
+        z_first = cross(0)
+        w3_scales = keep.tile([P, N], U8, name="w3_scales", align_bytes=64)
+        w3_mx.extend(quantize_tiles("w3_codes", w3_rounded[:], w3_scales[:]))
+        project_h(0, z_first)
+        project_h(1, cross(1))
 
         out_rows = out.rearrange("(p t) s -> p t s", t=PACK)
         gates = {}

@@ -63,9 +63,9 @@ def tile_picked_twlcrossbhopd_none_p_kernel(tc, x_words, x_scales, w1, w2, gn, w
         nc.sync.dma_start(table_words[:], x_words[0].rearrange("p c r -> p (c r)").bitcast(I32))
         offs_sb = load_list("offs_sb", offs)
         two_sb = load_list("two_sb", two)
+        n1_sb = load_list("n1_sb", n1)
         w1_raw = load_weight("w1_raw", w1)
         w2_raw = load_weight("w2_raw", w2)
-        n1_sb = load_list("n1_sb", n1)
         n2_sb = load_list("n2_sb", n2)
         gain = keep.tile([P, PACK], F32, name="gain")
         nc.sync.dma_start(gain[:], gn.rearrange("(p t) o -> p (t o)", t=PACK))
@@ -159,9 +159,9 @@ def tile_picked_twlcrossbhopd_none_p_kernel(tc, x_words, x_scales, w1, w2, gn, w
                     nc.vector.tensor_tensor(right[:, t, :], y_sb[t][:].indirect(entries(n1_sb, half)), d_sb[t][:, places(half)], MULT)
             z = keep.tile([P, HALF, PACK], BF16, name="z%d" % half, align_bytes=64)
             nc.vector.tensor_tensor(
-                z[:].rearrange("p (c i) t -> p c t i", i=4),
-                left[:].rearrange("p t (c i) -> p c t i", i=4),
-                right[:].rearrange("p t (c i) -> p c t i", i=4),
+                z[:].rearrange("p (c i) t -> p c t i", i=2),
+                left[:].rearrange("p t (c i) -> p c t i", i=2),
+                right[:].rearrange("p t (c i) -> p c t i", i=2),
                 SUBTRACT,
             )
             return z

@@ -19,10 +19,13 @@ SIGMOID = mybir.ActivationFunctionType.Sigmoid
 
 P = 128
 PACK = 4
-HALF = S // 2
+QUADRANT = 32
 LIST_ROWS = 16
-Y_BANKS = "aabc"
-D_BANKS = "bcde"
+HALF = S // 2
+STEP = 2
+
+Y_BANKS = "acbd"
+D_BANKS = "bdef"
 H_BANKS = ["aceg", "bdfh"]
 
 
@@ -37,8 +40,8 @@ def tile_picked_twlcrossbhopd_none_p_kernel(tc, x_words, x_scales, w1, w2, gn, w
             nc.sync.dma_start(tile[:], dram)
             return tile
 
-        def load_weight(name, dram):
-            tile = keep.tile([P, PACK, H], F32, name=name)
+        def load_weight(buffer, dram):
+            tile = keep.tile([P, PACK, H], F32, name=buffer)
             nc.sync.dma_start(tile[:], dram.rearrange("(p j) c -> p j c", j=PACK))
             return tile
 
@@ -51,8 +54,11 @@ def tile_picked_twlcrossbhopd_none_p_kernel(tc, x_words, x_scales, w1, w2, gn, w
 
         table_scales = keep.tile([P, T], U8, name="table_scales", align_bytes=64)
         nc.vector.memset(table_scales[:].bitcast(I32), 0)
-        for q in range(4):
-            nc.scalar.dma_start(table_scales[32 * q : 32 * q + 4, :].bitcast(I32), x_scales[0, 4 * q : 4 * q + 4, :].bitcast(I32))
+        for q in range(P // QUADRANT):
+            nc.scalar.dma_start(
+                table_scales[QUADRANT * q : QUADRANT * q + 4, :].bitcast(I32),
+                x_scales[0, 4 * q : 4 * q + 4, :].bitcast(I32),
+            )
 
         warm = keep.tile([P, 1], F32, name="warm")
         nc.vector.memset(warm[:], 0.0)
@@ -82,8 +88,8 @@ def tile_picked_twlcrossbhopd_none_p_kernel(tc, x_words, x_scales, w1, w2, gn, w
             nc.vector.tensor_copy(tile[:], table_scales[:].indirect(list_tile[:]))
             return tile
 
-        def round_pair(name, raw, pair, copy):
-            tile = keep.tile([P, 2, P * PACK], BF16, name=name, align_bytes=64)
+        def round_pair(buffer, raw, pair, copy):
+            tile = keep.tile([P, 2, P * PACK], BF16, name=buffer, align_bytes=64)
             copy(
                 tile[:].rearrange("p t (m j) -> p m j t", j=PACK),
                 raw[:].rearrange("p j (m t) -> p m j t", t=PACK)[:, :, :, 2 * pair : 2 * pair + 2],
@@ -106,34 +112,29 @@ def tile_picked_twlcrossbhopd_none_p_kernel(tc, x_words, x_scales, w1, w2, gn, w
         two_words = gather_words("two_words", two_sb)
         offs_scales = gather_scales("offs_scales", offs_sb)
         two_scales = gather_scales("two_scales", two_sb)
-        w1_rounded = [round_pair("w1_rounded%d" % pair, w1_raw, pair, nc.scalar.copy) for pair in range(2)]
-        w2_first = round_pair("w2_rounded0", w2_raw, 0, nc.scalar.copy)
+
+        w1_rounded = [round_pair("rounded%d" % pair, w1_raw, pair, nc.scalar.copy) for pair in range(2)]
         weight_scales = keep.tile([P, 2, H], U8, name="weight_scales", tag="table_scales", align_bytes=64)
         w1_mx = []
         for pair in range(2):
             w1_mx.extend(quantize_tiles("w1_codes%d" % pair, w1_rounded[pair][:], weight_scales[:, 0, 2 * pair * P : 2 * (pair + 1) * P]))
+
+        w2_first = round_pair("rounded0", w2_raw, 0, nc.vector.tensor_copy)
         w2_mx = []
         for t in range(2):
             w2_mx.extend(quantize_tiles("w2_codes%d" % t, w2_first[:, t : t + 1, :], weight_scales[:, 1, t * P : (t + 1) * P]))
-        w2_second = round_pair("w2_rounded0", w2_raw, 1, nc.vector.tensor_copy)
+        w2_second = round_pair("rounded0", w2_raw, 1, nc.vector.tensor_copy)
         w2_mx.extend(quantize_tiles("w2_codes2", w2_second[:], weight_scales[:, 1, 2 * P :]))
 
         y_sb = [keep.tile([P, S], F32, name="y%d" % t) for t in range(PACK)]
         d_sb = [keep.tile([P, S], F32, name="d%d" % t) for t in range(PACK)]
-
-        def project_y(t):
-            bank = psum.tile([P, S], F32, name="bank_" + Y_BANKS[t])
-            product(bank[:], w1_mx[t], offs_words[:], offs_scales[:])
-            nc.scalar.activation(y_sb[t][:], bank[:], COPY, scale=gain[:, t : t + 1])
-
-        def project_d(t):
-            bank = psum.tile([P, S], F32, name="bank_" + D_BANKS[t])
-            product(bank[:], w2_mx[t], two_words[:], two_scales[:])
-            nc.scalar.activation(d_sb[t][:], bank[:], COPY, scale=0.75)
-
         for t in range(PACK):
-            project_y(t)
-            project_d(t)
+            y_bank = psum.tile([P, S], F32, name="bank_" + Y_BANKS[t])
+            product(y_bank[:], w1_mx[t], offs_words[:], offs_scales[:])
+            nc.scalar.activation(y_sb[t][:], y_bank[:], COPY, scale=gain[:, t : t + 1])
+            d_bank = psum.tile([P, S], F32, name="bank_" + D_BANKS[t])
+            product(d_bank[:], w2_mx[t], two_words[:], two_scales[:])
+            nc.scalar.activation(d_sb[t][:], d_bank[:], COPY, scale=0.75)
 
         w3_raw = load_weight("w1_raw", w3)
         w3_rounded = keep.tile([P, PACK, P * PACK], BF16, name="w3_rounded", tag="two_words", align_bytes=64)
@@ -141,27 +142,23 @@ def tile_picked_twlcrossbhopd_none_p_kernel(tc, x_words, x_scales, w1, w2, gn, w
             w3_rounded[:].rearrange("p t (m j) -> p m j t", j=PACK),
             w3_raw[:].rearrange("p j (m t) -> p m j t", t=PACK),
         )
-        w3_mx = []
 
         h_sb = [keep.tile([P, S], F32, name="h%d" % t) for t in range(PACK)]
         h_plain = [keep.tile([P, S], F32, name="h_plain%d" % t) for t in range(PACK)]
 
-        def cross(half):
+        def cross(half, order, right_buffer):
             left = keep.tile([P, PACK, HALF], F32, name="left%d" % half)
-            right = keep.tile([P, PACK, HALF], F32, name="right%d" % half, tag=["right0", "two_words"][half], align_bytes=64)
-            steps = [(t, side) for t in range(PACK) for side in range(2)]
-            if half == 1:
-                steps = [(t, side) for side in range(2) for t in range(PACK)]
-            for t, side in steps:
-                if side == 0:
+            right = keep.tile([P, PACK, HALF], F32, name="right%d" % half, tag=right_buffer, align_bytes=64)
+            for t, side in order:
+                if side == "left":
                     nc.vector.tensor_tensor(left[:, t, :], d_sb[t][:].indirect(entries(n2_sb, half)), y_sb[t][:, places(half)], MULT)
                 else:
                     nc.vector.tensor_tensor(right[:, t, :], y_sb[t][:].indirect(entries(n1_sb, half)), d_sb[t][:, places(half)], MULT)
             z = keep.tile([P, HALF, PACK], BF16, name="z%d" % half, align_bytes=64)
             nc.vector.tensor_tensor(
-                z[:].rearrange("p (c i) t -> p c t i", i=2),
-                left[:].rearrange("p t (c i) -> p c t i", i=2),
-                right[:].rearrange("p t (c i) -> p c t i", i=2),
+                z[:].rearrange("p (c i) t -> p c t i", i=STEP),
+                left[:].rearrange("p t (c i) -> p c t i", i=STEP),
+                right[:].rearrange("p t (c i) -> p c t i", i=STEP),
                 SUBTRACT,
             )
             return z
@@ -170,37 +167,37 @@ def tile_picked_twlcrossbhopd_none_p_kernel(tc, x_words, x_scales, w1, w2, gn, w
             scales = keep.tile([P, HALF], U8, name="z_scales%d" % half, align_bytes=64)
             codes = quantize("z_codes%d" % half, z[:].rearrange("p c t -> p (c t)"), scales[:])
             for t in range(PACK):
-                bank = psum.tile([P, HALF], F32, name="bank_" + H_BANKS[half][t])
-                product(bank[:], w3_mx[t], codes[:], scales[:])
-                nc.scalar.copy(h_sb[t][:, places(half)], bank[:])
-                nc.scalar.copy(h_plain[t][:, places(half)], bank[:])
+                h_bank = psum.tile([P, HALF], F32, name="bank_" + H_BANKS[half][t])
+                product(h_bank[:], w3_mx[t], codes[:], scales[:])
+                nc.scalar.copy(h_sb[t][:, places(half)], h_bank[:])
+                nc.scalar.copy(h_plain[t][:, places(half)], h_bank[:])
 
-        z_first = cross(0)
+        sides = ["left", "right"]
+        z_first = cross(0, [(t, side) for t in range(PACK) for side in sides], "right0")
         w3_scales = keep.tile([P, N], U8, name="w3_scales", align_bytes=64)
-        w3_mx.extend(quantize_tiles("w3_codes", w3_rounded[:], w3_scales[:]))
+        w3_mx = quantize_tiles("w3_codes", w3_rounded[:], w3_scales[:])
         project_h(0, z_first)
-        project_h(1, cross(1))
+        project_h(1, cross(1, [(t, side) for side in sides for t in range(PACK)], "two_words"))
 
         out_rows = out.rearrange("(p t) s -> p t s", t=PACK)
-        gates = {}
 
-        def hop(t):
+        def two_hops(t):
             st = keep.tile([P, S], F32, name="st%d" % t)
             for half in range(2):
                 nc.vector.tensor_tensor(st[:, places(half)], h_sb[t][:].indirect(entries(n3_sb, half)), h_plain[t][:, places(half)], SUBTRACT)
             gate = keep.tile([P, S], F32, name="gate%d" % t)
             for half in range(2):
                 nc.scalar.activation(gate[:, places(half)], st[:].indirect(entries(n4_sb, half)), SIGMOID)
-            gates[t] = gate
+            return gate
 
-        def finish(t):
+        def finish(t, gate, pieces):
             result = keep.tile([P, S], F32, name="result%d" % t)
-            for cols in [slice(0, S)] if t < PACK - 1 else [places(0), places(1)]:
-                nc.vector.tensor_tensor(result[:, cols], gates[t][:, cols], h_plain[t][:, cols], MULT)
+            for cols in pieces:
+                nc.vector.tensor_tensor(result[:, cols], gate[:, cols], h_plain[t][:, cols], MULT)
                 nc.sync.dma_start(out_rows[:, t, cols], result[:, cols])
 
-        hop(0)
+        gates = [two_hops(0)]
         for t in range(1, PACK):
-            hop(t)
-            finish(t - 1)
-        finish(PACK - 1)
+            gates.append(two_hops(t))
+            finish(t - 1, gates[t - 1], [slice(0, S)])
+        finish(PACK - 1, gates[PACK - 1], [places(0), places(1)])

from contextlib import ExitStack

import concourse.mybir as mybir

K, T, S, H, N = 512, 2048, 512, 512, 512
FLOPS = 2 * (2 * K * H * S + H * N * S)

F32 = mybir.dt.float32
BF16 = mybir.dt.bfloat16
I32 = mybir.dt.int32
U32 = mybir.dt.uint32
U16 = mybir.dt.uint16
U8 = mybir.dt.uint8
FP8X4 = mybir.dt.float8_e4m3fn_x4
MULT = mybir.AluOpType.mult
SUBTRACT = mybir.AluOpType.subtract
COPY = mybir.ActivationFunctionType.Copy
SIGMOID = mybir.ActivationFunctionType.Sigmoid

P = 128
PACK = 4
QUADRANT = 32
LIST_ROWS = 16
HALF = S // 2
STEP = 2

Y_BANKS = "acbd"
D_BANKS = "bdef"
H_BANKS = ["aceg", "bdfh"]


def tile_picked_twlcrossbhopd_none_p_kernel(tc, x_words, x_scales, w1, w2, gn, w3, offs, two, n1, n2, n3, n4, out):
    nc = tc.nc
    with ExitStack() as ctx:
        keep = ctx.enter_context(tc.tile_pool(name="keep", bufs=1))
        psum = ctx.enter_context(tc.psum_pool(name="psum", bufs=1))

        def load_list(name, dram):
            tile = keep.tile([P, S // LIST_ROWS], U16, name=name)
            nc.sync.dma_start(tile[:], dram)
            return tile

        def load_weight(buffer, dram):
            tile = keep.tile([P, PACK, H], F32, name=buffer)
            nc.sync.dma_start(tile[:], dram.rearrange("(p j) c -> p j c", j=PACK))
            return tile

        def entries(list_tile, half):
            cols = HALF // LIST_ROWS
            return list_tile[:, half * cols : (half + 1) * cols]

        def places(half):
            return slice(half * HALF, (half + 1) * HALF)

        table_scales = keep.tile([P, T], U8, name="table_scales", align_bytes=64)
        nc.vector.memset(table_scales[:].bitcast(I32), 0)
        for q in range(P // QUADRANT):
            nc.scalar.dma_start(
                table_scales[QUADRANT * q : QUADRANT * q + 4, :].bitcast(I32),
                x_scales[0, 4 * q : 4 * q + 4, :].bitcast(I32),
            )

        warm = keep.tile([P, 1], F32, name="warm")
        nc.vector.memset(warm[:], 0.0)
        warmed = keep.tile([P, 1], F32, name="warmed")
        nc.scalar.activation(warmed[:], warm[:], SIGMOID)

        table_words = keep.tile([P, T], I32, name="table_words")
        nc.sync.dma_start(table_words[:], x_words[0].rearrange("p c r -> p (c r)").bitcast(I32))
        offs_sb = load_list("offs_sb", offs)
        two_sb = load_list("two_sb", two)
        n1_sb = load_list("n1_sb", n1)
        w1_raw = load_weight("w1_raw", w1)
        w2_raw = load_weight("w2_raw", w2)
        n2_sb = load_list("n2_sb", n2)
        gain = keep.tile([P, PACK], F32, name="gain")
        nc.sync.dma_start(gain[:], gn.rearrange("(p t) o -> p (t o)", t=PACK))
        n3_sb = load_list("n3_sb", n3)
        n4_sb = load_list("n4_sb", n4)

        def gather_words(name, list_tile):
            tile = keep.tile([P, S], U32, name=name, align_bytes=64)
            nc.vector.tensor_copy(tile[:], table_words[:].bitcast(U32).indirect(list_tile[:]))
            return tile

        def gather_scales(name, list_tile):
            tile = keep.tile([P, S], U8, name=name, align_bytes=64)
            nc.vector.tensor_copy(tile[:], table_scales[:].indirect(list_tile[:]))
            return tile

        def round_pair(buffer, raw, pair, copy):
            tile = keep.tile([P, 2, P * PACK], BF16, name=buffer, align_bytes=64)
            copy(
                tile[:].rearrange("p t (m j) -> p m j t", j=PACK),
                raw[:].rearrange("p j (m t) -> p m j t", t=PACK)[:, :, :, 2 * pair : 2 * pair + 2],
            )
            return tile

        def quantize(name, values, scales):
            codes = keep.tile([P, scales.shape[1]], U32, name=name, align_bytes=64)
            nc.vector.quantize_mx(codes[:].bitcast(FP8X4), scales, values)
            return codes

        def quantize_tiles(name, rounded, scales):
            codes = quantize(name, rounded.rearrange("p t c -> p (t c)"), scales)
            return [(codes[:, u * P : (u + 1) * P], scales[:, u * P : (u + 1) * P]) for u in range(rounded.shape[1])]

        def product(bank, weight, codes, scales):
            nc.tensor.matmul_mx(bank, weight[0].bitcast(FP8X4), weight[1], codes.bitcast(FP8X4), scales, start=True, stop=True)

        offs_words = gather_words("offs_words", offs_sb)
        two_words = gather_words("two_words", two_sb)
        offs_scales = gather_scales("offs_scales", offs_sb)
        two_scales = gather_scales("two_scales", two_sb)

        w1_rounded = [round_pair("rounded%d" % pair, w1_raw, pair, nc.scalar.copy) for pair in range(2)]
        weight_scales = keep.tile([P, 2, H], U8, name="weight_scales", tag="table_scales", align_bytes=64)
        w1_mx = []
        for pair in range(2):
            w1_mx.extend(quantize_tiles("w1_codes%d" % pair, w1_rounded[pair][:], weight_scales[:, 0, 2 * pair * P : 2 * (pair + 1) * P]))

        w2_first = round_pair("rounded0", w2_raw, 0, nc.vector.tensor_copy)
        w2_mx = []
        for t in range(2):
            w2_mx.extend(quantize_tiles("w2_codes%d" % t, w2_first[:, t : t + 1, :], weight_scales[:, 1, t * P : (t + 1) * P]))
        w2_second = round_pair("rounded0", w2_raw, 1, nc.vector.tensor_copy)
        w2_mx.extend(quantize_tiles("w2_codes2", w2_second[:], weight_scales[:, 1, 2 * P :]))

        y_sb = [keep.tile([P, S], F32, name="y%d" % t) for t in range(PACK)]
        d_sb = [keep.tile([P, S], F32, name="d%d" % t) for t in range(PACK)]
        for t in range(PACK):
            y_bank = psum.tile([P, S], F32, name="bank_" + Y_BANKS[t])
            product(y_bank[:], w1_mx[t], offs_words[:], offs_scales[:])
            nc.scalar.activation(y_sb[t][:], y_bank[:], COPY, scale=gain[:, t : t + 1])
            d_bank = psum.tile([P, S], F32, name="bank_" + D_BANKS[t])
            product(d_bank[:], w2_mx[t], two_words[:], two_scales[:])
            nc.scalar.activation(d_sb[t][:], d_bank[:], COPY, scale=0.75)

        w3_raw = load_weight("w1_raw", w3)
        w3_rounded = keep.tile([P, PACK, P * PACK], BF16, name="w3_rounded", tag="two_words", align_bytes=64)
        nc.scalar.copy(
            w3_rounded[:].rearrange("p t (m j) -> p m j t", j=PACK),
            w3_raw[:].rearrange("p j (m t) -> p m j t", t=PACK),
        )

        h_sb = [keep.tile([P, S], F32, name="h%d" % t) for t in range(PACK)]
        h_plain = [keep.tile([P, S], F32, name="h_plain%d" % t) for t in range(PACK)]

        def cross(half, order, right_buffer):
            left = keep.tile([P, PACK, HALF], F32, name="left%d" % half)
            right = keep.tile([P, PACK, HALF], F32, name="right%d" % half, tag=right_buffer, align_bytes=64)
            for t, side in order:
                if side == "left":
                    nc.vector.tensor_tensor(left[:, t, :], d_sb[t][:].indirect(entries(n2_sb, half)), y_sb[t][:, places(half)], MULT)
                else:
                    nc.vector.tensor_tensor(right[:, t, :], y_sb[t][:].indirect(entries(n1_sb, half)), d_sb[t][:, places(half)], MULT)
            z = keep.tile([P, HALF, PACK], BF16, name="z%d" % half, align_bytes=64)
            nc.vector.tensor_tensor(
                z[:].rearrange("p (c i) t -> p c t i", i=STEP),
                left[:].rearrange("p t (c i) -> p c t i", i=STEP),
                right[:].rearrange("p t (c i) -> p c t i", i=STEP),
                SUBTRACT,
            )
            return z

        def project_h(half, z):
            scales = keep.tile([P, HALF], U8, name="z_scales%d" % half, align_bytes=64)
            codes = quantize("z_codes%d" % half, z[:].rearrange("p c t -> p (c t)"), scales[:])
            for t in range(PACK):
                h_bank = psum.tile([P, HALF], F32, name="bank_" + H_BANKS[half][t])
                product(h_bank[:], w3_mx[t], codes[:], scales[:])
                nc.scalar.copy(h_sb[t][:, places(half)], h_bank[:])
                nc.scalar.copy(h_plain[t][:, places(half)], h_bank[:])

        sides = ["left", "right"]
        z_first = cross(0, [(t, side) for t in range(PACK) for side in sides], "right0")
        w3_scales = keep.tile([P, N], U8, name="w3_scales", align_bytes=64)
        w3_mx = quantize_tiles("w3_codes", w3_rounded[:], w3_scales[:])
        project_h(0, z_first)
        project_h(1, cross(1, [(t, side) for side in sides for t in range(PACK)], "two_words"))

        out_rows = out.rearrange("(p t) s -> p t s", t=PACK)

        def two_hops(t):
            st = keep.tile([P, S], F32, name="st%d" % t)
            for half in range(2):
                nc.vector.tensor_tensor(st[:, places(half)], h_sb[t][:].indirect(entries(n3_sb, half)), h_plain[t][:, places(half)], SUBTRACT)
            gate = keep.tile([P, S], F32, name="gate%d" % t)
            for half in range(2):
                nc.scalar.activation(gate[:, places(half)], st[:].indirect(entries(n4_sb, half)), SIGMOID)
            return gate

        def finish(t, gate, pieces):
            result = keep.tile([P, S], F32, name="result%d" % t)
            for cols in pieces:
                nc.vector.tensor_tensor(result[:, cols], gate[:, cols], h_plain[t][:, cols], MULT)
                nc.sync.dma_start(out_rows[:, t, cols], result[:, cols])

        gates = [two_hops(0)]
        for t in range(1, PACK):
            gates.append(two_hops(t))
            finish(t - 1, gates[t - 1], [slice(0, S)])
        finish(PACK - 1, gates[PACK - 1], [places(0), places(1)])
